import numpy as np, ml_dtypes
CORES = [65,73,81,89,97,105,113,121]
N = 8
KB, QP = 2, 256
MEM = [0]
def setup_inputs(rng):
    return {"q": rng.standard_normal((N, 128, QP), dtype=np.float32).astype(ml_dtypes.bfloat16), "k": rng.standard_normal((N, 128, KB * 128), dtype=np.float32).astype(ml_dtypes.bfloat16), "v": rng.standard_normal((N, 128, KB * 128), dtype=np.float32).astype(ml_dtypes.bfloat16)}
def setup_inputs_big(rng):
    d = setup_inputs(rng)
    for k in ("q", "k", "v"): d[k] = (d[k].astype(np.float32) * 1024.0).astype(d[k].dtype)
    return d
def setup_inputs_small(rng):
    d = setup_inputs(rng)
    for k in ("q", "k", "v"): d[k] = (d[k].astype(np.float32) * (1 / 1024.0)).astype(d[k].dtype)
    return d
def setup_inputs_apart(rng):
    d = setup_inputs(rng)
    f = (10.0 ** rng.permutation(np.linspace(-1.5, 1.5, N))).astype(np.float32).reshape(N, 1, 1)
    for k in ("q", "k", "v"): d[k] = (d[k].astype(np.float32) * f).astype(d[k].dtype)
    return d
def reference(q, k, v):
    Q, K, V = q.astype(np.float64), k.astype(np.float64), v.astype(np.float64)
    y = np.zeros((N, 128, QP))
    for r in range(N):
        for j in MEM:
            for b in range(KB):
                S = np.maximum(K[j][:, 128 * b:128 * b + 128].T @ Q[r], 0.0)
                y[r] += V[j][:, 128 * b:128 * b + 128].T @ S
    return {"y": y.astype(ml_dtypes.bfloat16 if q.dtype != np.float64 else np.float64)}

@@ -1,0 +1,126 @@
+from concourse.bass import DstId, RemoteDMATransfer
+from concourse.mybir import AluOpType
+
+SCRATCH = {
+    "kv": ("sbuf", [128, 512], "bfloat16"),
+    "qs": ("sbuf", [128, 256], "bfloat16"),
+    "zero": ("sbuf", [128, 256], "float32"),
+    "s0": ("sbuf", [128, 256], "bfloat16"),
+    "s1": ("sbuf", [128, 256], "bfloat16"),
+    "ys": ("sbuf", [128, 256], "bfloat16"),
+    "ps0": ("psum", [128, 512], "float32"),
+    "ps1": ("psum", [128, 512], "float32"),
+    "po": ("psum", [128, 512], "float32"),
+}
+SEMAPHORES = ["kin", "vin", "qin", "sent", "zf", "m0", "m1", "r0", "r1", "od", "cd", "st"]
+
+KW = 256
+
+
+def _count(mask):
+    return sum((mask >> e) & 1 for e in range(16))
+
+
+def _plan(T, topo):
+    cores = list(T.cores)
+    owner = cores[T.tables["MEM"][0]]
+    others = [c for c in cores if c != owner]
+    near = [c for c in others if topo.may_write(owner, c)]
+    far = [c for c in others if not topo.may_write(owner, c)]
+    far.sort(key=lambda c: 0 if topo.mates(topo.chip(owner), topo.chip(c)) else 1)
+    sends = []
+    if far:
+        idle = [c for c in range(topo.CHIPS * topo.CORES_PER_CHIP)
+                if topo.chip(c) == topo.chip(owner) and c not in cores and all(topo.may_write(c, d) for d in far)]
+        same = [c for c in idle if topo.die(c) == topo.die(owner)]
+        cross = [c for c in idle if topo.die(c) != topo.die(owner)]
+        h = (len(far) + 1) // 2
+        g1, g2 = far[:h], far[h:]
+        sends.append((owner, "k", [same[0], cross[0]]))
+        sends.append((owner, "v", [same[1], cross[1]]))
+        sends.append((same[0], "k", g1))
+        sends.append((cross[0], "k", g2))
+        sends.append((same[1], "v", g2))
+        sends.append((cross[1], "v", g1))
+    if near:
+        sends.append((owner, "kv", near))
+    return owner, [s for s in sends if s[2]]
+
+
+def _mask(topo, src, dsts):
+    m = topo.mask(src, dsts[0])
+    for d in dsts[1:]:
+        m &= topo.mask(src, d)
+    return m
+
+
+def _part(T, part):
+    if part == "k":
+        return T.kv[:, 0:KW]
+    if part == "v":
+        return T.kv[:, KW:2 * KW]
+    return T.kv[:, 0:2 * KW]
+
+
+def rank_program(g, core, T, topo):
+    owner, sends = _plan(T, topo)
+    rank = T.rank_of(core)
+    sem = T.sem
+
+    need = {"k": 0, "v": 0}
+    for src, part, dsts in sends:
+        if core in dsts:
+            need["v" if part == "v" else "k"] += _count(_mask(topo, src, dsts))
+    mine = [s for s in sends if s[0] == core]
+    if rank is None and not mine:
+        return
+
+    if core == owner:
+        g.sync.dma_start(T.kv[:, 0:KW], T.k[:, :]).then_inc(sem.kin, 16)
+        g.scalar.dma_start(T.kv[:, KW:2 * KW], T.v[:, :]).then_inc(sem.vin, 16)
+        need = {"k": 16, "v": 16}
+        g.sync.wait_ge(sem.kin, 16)
+        g.sync.wait_ge(sem.vin, 16)
+    if rank is not None:
+        g.sync.dma_start(T.qs[:, :], T.q[:, :]).then_inc(sem.qin, 16)
+        g.vector.memset(T.zero[:, :], 0.0).then_inc(sem.zf, 1)
+
+    left = 0
+    for src, part, dsts in mine:
+        if part in ("k", "kv"):
+            g.wait_ge(sem.kin, need["k"])
+        if part in ("v", "kv") and need["v"]:
+            g.wait_ge(sem.vin, need["v"])
+        m = _mask(topo, core, dsts)
+        ids = [DstId(rid=topo.addr(d)[0], pnc=topo.addr(d)[1]) for d in dsts]
+        g.remote_dma_fused(
+            [RemoteDMATransfer(dst_ids=ids, dma_engine_mask=m, remote_sem=(sem.vin if part == "v" else sem.kin),
+                               srcs=[_part(T, part)], dsts=[_part(T, part) for _ in dsts])],
+            local_sem=sem.sent)
+        left += _count(m)
+    if left:
+        g.wait_ge(sem.sent, left)
+    if rank is None:
+        return
+
+    te, ve = g.tensor, g.vector
+    te.wait_ge(sem.qin, 16)
+    te.wait_ge(sem.kin, need["k"])
+    te.matmul(T.ps0[:, 0:256], T.kv[:, 0:128], T.qs[:, :], True, True).then_inc(sem.m0, 1)
+    te.matmul(T.ps1[:, 0:256], T.kv[:, 128:256], T.qs[:, :], True, True).then_inc(sem.m1, 1)
+    ve.wait_ge(sem.zf, 1)
+    ve.wait_ge(sem.m0, 1)
+    ve.tensor_tensor(T.s0[:, :], T.ps0[:, 0:256], T.zero[:, :], AluOpType.max).then_inc(sem.r0, 1)
+    ve.wait_ge(sem.m1, 1)
+    ve.tensor_tensor(T.s1[:, :], T.ps1[:, 0:256], T.zero[:, :], AluOpType.max).then_inc(sem.r1, 1)
+    if need["v"]:
+        te.wait_ge(sem.vin, need["v"])
+    te.wait_ge(sem.r0, 1)
+    te.matmul(T.po[:, 0:256], T.kv[:, KW:KW + 128], T.s0[:, :], True, False)
+    te.wait_ge(sem.r1, 1)
+    te.matmul(T.po[:, 0:256], T.kv[:, KW + 128:KW + 256], T.s1[:, :], False, True).then_inc(sem.od, 1)
+    ve.wait_ge(sem.od, 1)
+    ve.tensor_copy(T.ys[:, :], T.po[:, 0:256]).then_inc(sem.cd, 1)
+    g.sync.wait_ge(sem.cd, 1)
+    g.sync.dma_start(T.y[:, :], T.ys[:, :]).then_inc(sem.st, 16)
+    g.sync.wait_ge(sem.st, 16)

@@ -2,6 +2,9 @@ from concourse.bass import DstId, RemoteDMATransfer
 from concourse.mybir import AluOpType
 
 SCRATCH = {
+    "kd0": ("dram", [128, 128], "bfloat16"),
+    "kd1": ("dram", [128, 128], "bfloat16"),
+    "vd": ("dram", [128, 256], "bfloat16"),
     "kv": ("sbuf", [128, 512], "bfloat16"),
     "qs": ("sbuf", [128, 256], "bfloat16"),
     "zero": ("sbuf", [128, 256], "float32"),
@@ -10,15 +13,23 @@ SCRATCH = {
     "ys": ("sbuf", [128, 256], "bfloat16"),
     "ps0": ("psum", [128, 512], "float32"),
     "ps1": ("psum", [128, 512], "float32"),
-    "po": ("psum", [128, 512], "float32"),
+    "po0": ("psum", [128, 512], "float32"),
+    "po1": ("psum", [128, 512], "float32"),
+    "po2": ("psum", [128, 512], "float32"),
 }
-SEMAPHORES = ["kin", "vin", "qin", "sent", "zf", "m0", "m1", "r0", "r1", "od", "cd", "st"]
-
-KW = 256
+SEMAPHORES = ["kl0", "kl1", "vl", "ksb", "vsb", "qin", "k0in", "k1in", "vin", "sent", "zf", "a0", "a1",
+              "r0", "r1a", "r1b", "od0", "od1", "od2", "cd0", "cd1", "st0", "st1"]
 
 
 def _count(mask):
     return sum((mask >> e) & 1 for e in range(16))
+
+
+def _common(topo, src, dsts):
+    m = topo.mask(src, dsts[0])
+    for d in dsts[1:]:
+        m &= topo.mask(src, d)
+    return m
 
 
 def _plan(T, topo):
@@ -27,100 +38,128 @@ def _plan(T, topo):
     others = [c for c in cores if c != owner]
     near = [c for c in others if topo.may_write(owner, c)]
     far = [c for c in others if not topo.may_write(owner, c)]
-    far.sort(key=lambda c: 0 if topo.mates(topo.chip(owner), topo.chip(c)) else 1)
-    sends = []
-    if far:
-        idle = [c for c in range(topo.CHIPS * topo.CORES_PER_CHIP)
-                if topo.chip(c) == topo.chip(owner) and c not in cores and all(topo.may_write(c, d) for d in far)]
-        same = [c for c in idle if topo.die(c) == topo.die(owner)]
-        cross = [c for c in idle if topo.die(c) != topo.die(owner)]
-        h = (len(far) + 1) // 2
-        g1, g2 = far[:h], far[h:]
-        sends.append((owner, "k", [same[0], cross[0]]))
-        sends.append((owner, "v", [same[1], cross[1]]))
-        sends.append((same[0], "k", g1))
-        sends.append((cross[0], "k", g2))
-        sends.append((same[1], "v", g2))
-        sends.append((cross[1], "v", g1))
-    if near:
-        sends.append((owner, "kv", near))
-    return owner, [s for s in sends if s[2]]
+    idle = [c for c in range(topo.CHIPS * topo.CORES_PER_CHIP)
+            if topo.chip(c) == topo.chip(owner) and c not in cores]
+    port = [c for c in idle if all(topo.may_write(c, d) for d in far)]
+    kto = {}
+    for c, d in zip(port, far):
+        kto[c] = d
+    vto = dict(kto)
+    a = [c for c in kto if topo.mates(topo.chip(owner), topo.chip(kto[c]))]
+    b = [c for c in kto if a and topo.die(c) != topo.die(a[0])]
+    if a and b:
+        vto[a[0]], vto[b[0]] = kto[b[0]], kto[a[0]]
+    spare = [c for c in idle if c not in kto]
+    pick = ([c for c in spare if topo.die(c) == topo.die(owner)][:1]
+            + [c for c in spare if topo.die(c) != topo.die(owner)][:1])
+    direct = list(near)
+    for c in pick:
+        if len(direct) > 1:
+            kto[c] = direct.pop()
+            vto[c] = kto[c]
+    return owner, kto, vto, direct
 
 
-def _mask(topo, src, dsts):
-    m = topo.mask(src, dsts[0])
-    for d in dsts[1:]:
-        m &= topo.mask(src, d)
-    return m
-
-
-def _part(T, part):
-    if part == "k":
-        return T.kv[:, 0:KW]
-    if part == "v":
-        return T.kv[:, KW:2 * KW]
-    return T.kv[:, 0:2 * KW]
+def _ids(topo, dsts):
+    return [DstId(rid=topo.addr(d)[0], pnc=topo.addr(d)[1]) for d in dsts]
 
 
 def rank_program(g, core, T, topo):
-    owner, sends = _plan(T, topo)
+    owner, kto, vto, direct = _plan(T, topo)
     rank = T.rank_of(core)
     sem = T.sem
+    if rank is None and core not in kto:
+        return
+    relays = list(kto)
+    on_chip = _common(topo, owner, relays)
+    off_chip = _common(topo, owner, direct)
 
-    need = {"k": 0, "v": 0}
-    for src, part, dsts in sends:
-        if core in dsts:
-            need["v" if part == "v" else "k"] += _count(_mask(topo, src, dsts))
-    mine = [s for s in sends if s[0] == core]
-    if rank is None and not mine:
+    def write(src, dst, dsts, m, rsem):
+        g.remote_dma_fused(
+            [RemoteDMATransfer(dst_ids=_ids(topo, dsts), dma_engine_mask=m, remote_sem=rsem,
+                               srcs=[src], dsts=[dst for _ in dsts])],
+            local_sem=sem.sent)
+        return _count(m)
+
+    if core in kto:
+        m = _common(topo, core, [kto[core], vto[core]])
+        g.wait_ge(sem.k0in, _count(on_chip))
+        left = write(T.kd0[:, :], T.kv[:, 0:128], [kto[core]], m, sem.k0in)
+        g.wait_ge(sem.k1in, _count(on_chip))
+        left += write(T.kd1[:, :], T.kv[:, 128:256], [kto[core]], m, sem.k1in)
+        g.wait_ge(sem.vin, _count(on_chip))
+        left += write(T.vd[:, :], T.kv[:, 256:512], [vto[core]], m, sem.vin)
+        g.wait_ge(sem.sent, left)
         return
 
     if core == owner:
-        g.sync.dma_start(T.kv[:, 0:KW], T.k[:, :]).then_inc(sem.kin, 16)
-        g.scalar.dma_start(T.kv[:, KW:2 * KW], T.v[:, :]).then_inc(sem.vin, 16)
-        need = {"k": 16, "v": 16}
-        g.sync.wait_ge(sem.kin, 16)
-        g.sync.wait_ge(sem.vin, 16)
-    if rank is not None:
-        g.sync.dma_start(T.qs[:, :], T.q[:, :]).then_inc(sem.qin, 16)
-        g.vector.memset(T.zero[:, :], 0.0).then_inc(sem.zf, 1)
+        g.sync.dma_start(T.kd0[:, :], T.k[:, 0:128]).then_inc(sem.kl0, 16)
+        g.sync.dma_start(T.kd1[:, :], T.k[:, 128:256]).then_inc(sem.kl1, 16)
+        g.sync.dma_start(T.kv[:, 0:256], T.k[:, :]).then_inc(sem.ksb, 16)
+        g.scalar.wait_ge(sem.kl0, 16)
+        g.scalar.dma_start(T.vd[:, :], T.v[:, :]).then_inc(sem.vl, 16)
+        g.scalar.dma_start(T.kv[:, 256:512], T.v[:, :]).then_inc(sem.vsb, 16)
+    g.sync.dma_start(T.qs[:, :], T.q[:, :]).then_inc(sem.qin, 16)
+    g.vector.memset(T.zero[:, :], 0.0).then_inc(sem.zf, 1)
 
-    left = 0
-    for src, part, dsts in mine:
-        if part in ("k", "kv"):
-            g.wait_ge(sem.kin, need["k"])
-        if part in ("v", "kv") and need["v"]:
-            g.wait_ge(sem.vin, need["v"])
-        m = _mask(topo, core, dsts)
-        ids = [DstId(rid=topo.addr(d)[0], pnc=topo.addr(d)[1]) for d in dsts]
-        g.remote_dma_fused(
-            [RemoteDMATransfer(dst_ids=ids, dma_engine_mask=m, remote_sem=(sem.vin if part == "v" else sem.kin),
-                               srcs=[_part(T, part)], dsts=[_part(T, part) for _ in dsts])],
-            local_sem=sem.sent)
-        left += _count(m)
-    if left:
+    if core == owner:
+        g.wait_ge(sem.kl0, 16)
+        left = write(T.kd0[:, :], T.kd0[:, :], relays, on_chip, sem.k0in)
+        g.wait_ge(sem.kl1, 16)
+        left += write(T.kd1[:, :], T.kd1[:, :], relays, on_chip, sem.k1in)
+        g.wait_ge(sem.vl, 16)
+        left += write(T.vd[:, :], T.vd[:, :], relays, on_chip, sem.vin)
+        g.wait_ge(sem.ksb, 16)
+        g.wait_ge(sem.vsb, 16)
+        left += write(T.kv[:, :], T.kv[:, :], direct, off_chip, sem.k0in)
         g.wait_ge(sem.sent, left)
-    if rank is None:
-        return
+
+    if core == owner:
+        w0, w1, wv = [(sem.ksb, 16)], [], [(sem.vsb, 16)]
+    elif core in direct:
+        w0, w1, wv = [(sem.k0in, _count(off_chip))], [], []
+    else:
+        ks = [c for c in relays if kto[c] == core][0]
+        vs = [c for c in relays if vto[c] == core][0]
+        nk = _count(_common(topo, ks, [kto[ks], vto[ks]]))
+        nv = _count(_common(topo, vs, [kto[vs], vto[vs]]))
+        w0, w1, wv = [(sem.k0in, nk)], [(sem.k1in, nk)], [(sem.vin, nv)]
 
     te, ve = g.tensor, g.vector
+    v0, v1 = T.kv[:, 256:384], T.kv[:, 384:512]
     te.wait_ge(sem.qin, 16)
-    te.wait_ge(sem.kin, need["k"])
-    te.matmul(T.ps0[:, 0:256], T.kv[:, 0:128], T.qs[:, :], True, True).then_inc(sem.m0, 1)
-    te.matmul(T.ps1[:, 0:256], T.kv[:, 128:256], T.qs[:, :], True, True).then_inc(sem.m1, 1)
+    for s, n in w0:
+        te.wait_ge(s, n)
+    te.matmul(T.ps0[:, 0:256], T.kv[:, 0:128], T.qs[:, :], True, True).then_inc(sem.a0, 1)
+    for s, n in w1:
+        te.wait_ge(s, n)
+    te.matmul(T.ps1[:, 0:256], T.kv[:, 128:256], T.qs[:, :], True, True).then_inc(sem.a1, 1)
     ve.wait_ge(sem.zf, 1)
-    ve.wait_ge(sem.m0, 1)
+    ve.wait_ge(sem.a0, 1)
     ve.tensor_tensor(T.s0[:, :], T.ps0[:, 0:256], T.zero[:, :], AluOpType.max).then_inc(sem.r0, 1)
-    ve.wait_ge(sem.m1, 1)
-    ve.tensor_tensor(T.s1[:, :], T.ps1[:, 0:256], T.zero[:, :], AluOpType.max).then_inc(sem.r1, 1)
-    if need["v"]:
-        te.wait_ge(sem.vin, need["v"])
+    ve.wait_ge(sem.a1, 1)
+    ve.tensor_tensor(T.s1[:, 0:128], T.ps1[:, 0:128], T.zero[:, 0:128], AluOpType.max).then_inc(sem.r1a, 1)
+    ve.tensor_tensor(T.s1[:, 128:256], T.ps1[:, 128:256], T.zero[:, 128:256], AluOpType.max).then_inc(sem.r1b, 1)
+    for s, n in wv:
+        te.wait_ge(s, n)
     te.wait_ge(sem.r0, 1)
-    te.matmul(T.po[:, 0:256], T.kv[:, KW:KW + 128], T.s0[:, :], True, False)
-    te.wait_ge(sem.r1, 1)
-    te.matmul(T.po[:, 0:256], T.kv[:, KW + 128:KW + 256], T.s1[:, :], False, True).then_inc(sem.od, 1)
-    ve.wait_ge(sem.od, 1)
-    ve.tensor_copy(T.ys[:, :], T.po[:, 0:256]).then_inc(sem.cd, 1)
-    g.sync.wait_ge(sem.cd, 1)
-    g.sync.dma_start(T.y[:, :], T.ys[:, :]).then_inc(sem.st, 16)
-    g.sync.wait_ge(sem.st, 16)
+    te.matmul(T.po0[:, 0:128], v0, T.s0[:, 0:128], True, False)
+    te.wait_ge(sem.r1a, 1)
+    te.matmul(T.po0[:, 0:128], v1, T.s1[:, 0:128], False, True).then_inc(sem.od0, 1)
+    te.matmul(T.po1[:, 0:64], v0, T.s0[:, 128:192], True, False)
+    te.wait_ge(sem.r1b, 1)
+    te.matmul(T.po1[:, 0:64], v1, T.s1[:, 128:192], False, True).then_inc(sem.od1, 1)
+    te.matmul(T.po2[:, 0:64], v0, T.s0[:, 192:256], True, False)
+    te.matmul(T.po2[:, 0:64], v1, T.s1[:, 192:256], False, True).then_inc(sem.od2, 1)
+    ve.wait_ge(sem.od0, 1)
+    ve.tensor_copy(T.ys[:, 0:128], T.po0[:, 0:128]).then_inc(sem.cd0, 1)
+    ve.wait_ge(sem.od1, 1)
+    ve.tensor_copy(T.ys[:, 128:192], T.po1[:, 0:64]).then_inc(sem.cd1, 1)
+    ve.wait_ge(sem.od2, 1)
+    ve.tensor_copy(T.ys[:, 192:256], T.po2[:, 0:64]).then_inc(sem.cd1, 1)
+    g.scalar.wait_ge(sem.cd0, 1)
+    g.scalar.dma_start(T.y[:, 0:128], T.ys[:, 0:128]).then_inc(sem.st0, 16)
+    g.sync.wait_ge(sem.cd1, 2)
+    g.sync.dma_start(T.y[:, 128:256], T.ys[:, 128:256]).then_inc(sem.st1, 16)
+    g.scalar.wait_ge(sem.st0, 16)
+    g.sync.wait_ge(sem.st1, 16)

@@ -1,28 +1,40 @@
 from concourse.bass import DstId, RemoteDMATransfer
-from concourse.mybir import AluOpType
+from concourse.mybir import AluOpType, ActivationFunctionType
 
+HEAD = 8
 SCRATCH = {
+    "vh": ("dram", [128, HEAD], "bfloat16"),
     "kd0": ("dram", [128, 128], "bfloat16"),
     "kd1": ("dram", [128, 128], "bfloat16"),
-    "vd": ("dram", [128, 256], "bfloat16"),
+    "vd0": ("dram", [128, 128 - HEAD], "bfloat16"),
+    "vd1": ("dram", [128, 128], "bfloat16"),
     "kv": ("sbuf", [128, 512], "bfloat16"),
     "qs": ("sbuf", [128, 256], "bfloat16"),
-    "zero": ("sbuf", [128, 256], "float32"),
+    "zero": ("sbuf", [128, 128], "float32"),
     "s0": ("sbuf", [128, 256], "bfloat16"),
     "s1": ("sbuf", [128, 256], "bfloat16"),
     "ys": ("sbuf", [128, 256], "bfloat16"),
-    "ps0": ("psum", [128, 512], "float32"),
-    "ps1": ("psum", [128, 512], "float32"),
+    "ps00": ("psum", [128, 512], "float32"),
+    "ps10": ("psum", [128, 512], "float32"),
+    "ps01": ("psum", [128, 512], "float32"),
+    "ps11": ("psum", [128, 512], "float32"),
     "po0": ("psum", [128, 512], "float32"),
     "po1": ("psum", [128, 512], "float32"),
     "po2": ("psum", [128, 512], "float32"),
 }
-SEMAPHORES = ["kl0", "kl1", "vl", "ksb", "vsb", "qin", "k0in", "k1in", "vin", "sent", "zf", "a0", "a1",
-              "r0", "r1a", "r1b", "od0", "od1", "od2", "cd0", "cd1", "st0", "st1"]
+SEMAPHORES = ["hl", "kl0", "kl1", "vl0", "vl1", "ksb", "vsb", "qin", "hin", "k0in", "k1in", "v0in", "v1in", "hsb",
+              "sent", "zf", "a00", "a10", "a01", "a11", "r00", "r10", "r01", "r11",
+              "od0", "od1", "od2", "cd0", "cd1", "st0", "st1"]
 
 
 def _count(mask):
     return sum((mask >> e) & 1 for e in range(16))
+
+
+def _halves(mask):
+    es = [e for e in range(16) if (mask >> e) & 1]
+    h = len(es) // 2
+    return sum(1 << e for e in es[:h]), sum(1 << e for e in es[h:])
 
 
 def _common(topo, src, dsts):
@@ -72,7 +84,9 @@ def rank_program(g, core, T, topo):
         return
     relays = list(kto)
     on_chip = _common(topo, owner, relays)
+    head = _halves(_halves(on_chip)[1])[1]
     off_chip = _common(topo, owner, direct)
+    n_on, n_off = _count(on_chip), _count(off_chip)
 
     def write(src, dst, dsts, m, rsem):
         g.remote_dma_fused(
@@ -83,73 +97,98 @@ def rank_program(g, core, T, topo):
 
     if core in kto:
         m = _common(topo, core, [kto[core], vto[core]])
-        g.wait_ge(sem.k0in, _count(on_chip))
-        left = write(T.kd0[:, :], T.kv[:, 0:128], [kto[core]], m, sem.k0in)
-        g.wait_ge(sem.k1in, _count(on_chip))
+        g.wait_ge(sem.hin, _count(head))
+        left = write(T.vh[:, :], T.vh[:, :], [kto[core]], m, sem.hin)
+        g.wait_ge(sem.k0in, n_on)
+        left += write(T.kd0[:, :], T.kv[:, 0:128], [kto[core]], m, sem.k0in)
+        g.wait_ge(sem.k1in, n_on)
         left += write(T.kd1[:, :], T.kv[:, 128:256], [kto[core]], m, sem.k1in)
-        g.wait_ge(sem.vin, _count(on_chip))
-        left += write(T.vd[:, :], T.kv[:, 256:512], [vto[core]], m, sem.vin)
+        g.wait_ge(sem.v0in, n_on)
+        left += write(T.vd0[:, :], T.kv[:, 256 + HEAD:384], [vto[core]], m, sem.v0in)
+        g.wait_ge(sem.v1in, n_on)
+        left += write(T.vd1[:, :], T.kv[:, 384:512], [vto[core]], m, sem.v1in)
         g.wait_ge(sem.sent, left)
         return
 
     if core == owner:
+        g.sync.dma_start(T.vh[:, :], T.v[:, 0:HEAD]).then_inc(sem.hl, 16)
         g.sync.dma_start(T.kd0[:, :], T.k[:, 0:128]).then_inc(sem.kl0, 16)
         g.sync.dma_start(T.kd1[:, :], T.k[:, 128:256]).then_inc(sem.kl1, 16)
         g.sync.dma_start(T.kv[:, 0:256], T.k[:, :]).then_inc(sem.ksb, 16)
-        g.scalar.wait_ge(sem.kl0, 16)
-        g.scalar.dma_start(T.vd[:, :], T.v[:, :]).then_inc(sem.vl, 16)
+        g.scalar.wait_ge(sem.hl, 16)
+        g.scalar.dma_start(T.vd0[:, :], T.v[:, HEAD:128]).then_inc(sem.vl0, 16)
+        g.scalar.dma_start(T.vd1[:, :], T.v[:, 128:256]).then_inc(sem.vl1, 16)
         g.scalar.dma_start(T.kv[:, 256:512], T.v[:, :]).then_inc(sem.vsb, 16)
     g.sync.dma_start(T.qs[:, :], T.q[:, :]).then_inc(sem.qin, 16)
     g.vector.memset(T.zero[:, :], 0.0).then_inc(sem.zf, 1)
 
     if core == owner:
+        g.wait_ge(sem.hl, 16)
+        left = write(T.vh[:, :], T.vh[:, :], relays, head, sem.hin)
         g.wait_ge(sem.kl0, 16)
-        left = write(T.kd0[:, :], T.kd0[:, :], relays, on_chip, sem.k0in)
+        left += write(T.kd0[:, :], T.kd0[:, :], relays, on_chip, sem.k0in)
         g.wait_ge(sem.kl1, 16)
         left += write(T.kd1[:, :], T.kd1[:, :], relays, on_chip, sem.k1in)
-        g.wait_ge(sem.vl, 16)
-        left += write(T.vd[:, :], T.vd[:, :], relays, on_chip, sem.vin)
+        g.wait_ge(sem.vl0, 16)
+        left += write(T.vd0[:, :], T.vd0[:, :], relays, on_chip, sem.v0in)
+        g.wait_ge(sem.vl1, 16)
+        left += write(T.vd1[:, :], T.vd1[:, :], relays, on_chip, sem.v1in)
         g.wait_ge(sem.ksb, 16)
+        left += write(T.kv[:, 0:256], T.kv[:, 0:256], direct, off_chip, sem.k0in)
         g.wait_ge(sem.vsb, 16)
-        left += write(T.kv[:, :], T.kv[:, :], direct, off_chip, sem.k0in)
+        left += write(T.kv[:, 256:384], T.kv[:, 256:384], direct, off_chip, sem.v0in)
+        left += write(T.kv[:, 384:512], T.kv[:, 384:512], direct, off_chip, sem.v1in)
         g.wait_ge(sem.sent, left)
 
     if core == owner:
-        w0, w1, wv = [(sem.ksb, 16)], [], [(sem.vsb, 16)]
+        wk0, wk1, wv0, wv1 = [(sem.ksb, 16)], [], [(sem.vsb, 16)], []
     elif core in direct:
-        w0, w1, wv = [(sem.k0in, _count(off_chip))], [], []
+        wk0, wk1, wv0, wv1 = [(sem.k0in, n_off)], [], [(sem.v0in, n_off)], [(sem.v1in, n_off)]
     else:
         ks = [c for c in relays if kto[c] == core][0]
         vs = [c for c in relays if vto[c] == core][0]
         nk = _count(_common(topo, ks, [kto[ks], vto[ks]]))
         nv = _count(_common(topo, vs, [kto[vs], vto[vs]]))
-        w0, w1, wv = [(sem.k0in, nk)], [(sem.k1in, nk)], [(sem.vin, nv)]
+        g.sync.wait_ge(sem.hin, nk)
+        g.sync.dma_start(T.kv[:, 256:256 + HEAD], T.vh[:, :]).then_inc(sem.hsb, 16)
+        wk0, wk1 = [(sem.k0in, nk)], [(sem.k1in, nk)]
+        wv0, wv1 = [(sem.v0in, nv), (sem.hsb, 16)], [(sem.v1in, nv)]
 
-    te, ve = g.tensor, g.vector
+    te, ve, se = g.tensor, g.vector, g.scalar
+    k0, k1 = T.kv[:, 0:128], T.kv[:, 128:256]
     v0, v1 = T.kv[:, 256:384], T.kv[:, 384:512]
+    relu = ActivationFunctionType.Relu
     te.wait_ge(sem.qin, 16)
-    for s, n in w0:
+    for s, n in wk0:
         te.wait_ge(s, n)
-    te.matmul(T.ps0[:, 0:256], T.kv[:, 0:128], T.qs[:, :], True, True).then_inc(sem.a0, 1)
-    for s, n in w1:
+    te.matmul(T.ps00[:, 0:128], k0, T.qs[:, 0:128], True, True).then_inc(sem.a00, 1)
+    te.matmul(T.ps01[:, 0:128], k0, T.qs[:, 128:256], True, True).then_inc(sem.a01, 1)
+    for s, n in wk1:
         te.wait_ge(s, n)
-    te.matmul(T.ps1[:, 0:256], T.kv[:, 128:256], T.qs[:, :], True, True).then_inc(sem.a1, 1)
+    te.matmul(T.ps10[:, 0:128], k1, T.qs[:, 0:128], True, True).then_inc(sem.a10, 1)
+    te.matmul(T.ps11[:, 0:128], k1, T.qs[:, 128:256], True, True).then_inc(sem.a11, 1)
     ve.wait_ge(sem.zf, 1)
-    ve.wait_ge(sem.a0, 1)
-    ve.tensor_tensor(T.s0[:, :], T.ps0[:, 0:256], T.zero[:, :], AluOpType.max).then_inc(sem.r0, 1)
-    ve.wait_ge(sem.a1, 1)
-    ve.tensor_tensor(T.s1[:, 0:128], T.ps1[:, 0:128], T.zero[:, 0:128], AluOpType.max).then_inc(sem.r1a, 1)
-    ve.tensor_tensor(T.s1[:, 128:256], T.ps1[:, 128:256], T.zero[:, 128:256], AluOpType.max).then_inc(sem.r1b, 1)
-    for s, n in wv:
+    ve.wait_ge(sem.a00, 1)
+    ve.tensor_tensor(T.s0[:, 0:128], T.ps00[:, 0:128], T.zero[:, :], AluOpType.max).then_inc(sem.r00, 1)
+    se.wait_ge(sem.a01, 1)
+    se.activation(T.s0[:, 128:256], T.ps01[:, 0:128], relu).then_inc(sem.r01, 1)
+    ve.wait_ge(sem.a10, 1)
+    ve.tensor_tensor(T.s1[:, 0:128], T.ps10[:, 0:128], T.zero[:, :], AluOpType.max).then_inc(sem.r10, 1)
+    se.wait_ge(sem.a11, 1)
+    se.activation(T.s1[:, 128:256], T.ps11[:, 0:128], relu).then_inc(sem.r11, 1)
+    for s, n in wv0:
         te.wait_ge(s, n)
-    te.wait_ge(sem.r0, 1)
+    te.wait_ge(sem.r00, 1)
     te.matmul(T.po0[:, 0:128], v0, T.s0[:, 0:128], True, False)
-    te.wait_ge(sem.r1a, 1)
-    te.matmul(T.po0[:, 0:128], v1, T.s1[:, 0:128], False, True).then_inc(sem.od0, 1)
+    te.wait_ge(sem.r01, 1)
     te.matmul(T.po1[:, 0:64], v0, T.s0[:, 128:192], True, False)
-    te.wait_ge(sem.r1b, 1)
-    te.matmul(T.po1[:, 0:64], v1, T.s1[:, 128:192], False, True).then_inc(sem.od1, 1)
     te.matmul(T.po2[:, 0:64], v0, T.s0[:, 192:256], True, False)
+    for s, n in wv1:
+        te.wait_ge(s, n)
+    te.wait_ge(sem.r10, 1)
+    te.matmul(T.po0[:, 0:128], v1, T.s1[:, 0:128], False, True).then_inc(sem.od0, 1)
+    te.wait_ge(sem.r11, 1)
+    te.matmul(T.po1[:, 0:64], v1, T.s1[:, 128:192], False, True).then_inc(sem.od1, 1)
     te.matmul(T.po2[:, 0:64], v1, T.s1[:, 192:256], False, True).then_inc(sem.od2, 1)
     ve.wait_ge(sem.od0, 1)
     ve.tensor_copy(T.ys[:, 0:128], T.po0[:, 0:128]).then_inc(sem.cd0, 1)

from concourse.bass import DstId, RemoteDMATransfer
from concourse.mybir import AluOpType, ActivationFunctionType

HEAD = 8
SCRATCH = {
    "vh": ("dram", [128, HEAD], "bfloat16"),
    "kd0": ("dram", [128, 128], "bfloat16"),
    "kd1": ("dram", [128, 128], "bfloat16"),
    "vd0": ("dram", [128, 128 - HEAD], "bfloat16"),
    "vd1": ("dram", [128, 128], "bfloat16"),
    "kv": ("sbuf", [128, 512], "bfloat16"),
    "qs": ("sbuf", [128, 256], "bfloat16"),
    "zero": ("sbuf", [128, 128], "float32"),
    "s0": ("sbuf", [128, 256], "bfloat16"),
    "s1": ("sbuf", [128, 256], "bfloat16"),
    "ys": ("sbuf", [128, 256], "bfloat16"),
    "ps00": ("psum", [128, 512], "float32"),
    "ps10": ("psum", [128, 512], "float32"),
    "ps01": ("psum", [128, 512], "float32"),
    "ps11": ("psum", [128, 512], "float32"),
    "po0": ("psum", [128, 512], "float32"),
    "po1": ("psum", [128, 512], "float32"),
    "po2": ("psum", [128, 512], "float32"),
}
SEMAPHORES = ["hl", "kl0", "kl1", "vl0", "vl1", "ksb", "vsb", "qin", "hin", "k0in", "k1in", "v0in", "v1in", "hsb",
              "sent", "zf", "a00", "a10", "a01", "a11", "r00", "r10", "r01", "r11",
              "od0", "od1", "od2", "cd0", "cd1", "st0", "st1"]


def _count(mask):
    return sum((mask >> e) & 1 for e in range(16))


def _halves(mask):
    es = [e for e in range(16) if (mask >> e) & 1]
    h = len(es) // 2
    return sum(1 << e for e in es[:h]), sum(1 << e for e in es[h:])


def _common(topo, src, dsts):
    m = topo.mask(src, dsts[0])
    for d in dsts[1:]:
        m &= topo.mask(src, d)
    return m


def _plan(T, topo):
    cores = list(T.cores)
    owner = cores[T.tables["MEM"][0]]
    others = [c for c in cores if c != owner]
    near = [c for c in others if topo.may_write(owner, c)]
    far = [c for c in others if not topo.may_write(owner, c)]
    idle = [c for c in range(topo.CHIPS * topo.CORES_PER_CHIP)
            if topo.chip(c) == topo.chip(owner) and c not in cores]
    port = [c for c in idle if all(topo.may_write(c, d) for d in far)]
    kto = {}
    for c, d in zip(port, far):
        kto[c] = d
    vto = dict(kto)
    a = [c for c in kto if topo.mates(topo.chip(owner), topo.chip(kto[c]))]
    b = [c for c in kto if a and topo.die(c) != topo.die(a[0])]
    if a and b:
        vto[a[0]], vto[b[0]] = kto[b[0]], kto[a[0]]
    spare = [c for c in idle if c not in kto]
    pick = ([c for c in spare if topo.die(c) == topo.die(owner)][:1]
            + [c for c in spare if topo.die(c) != topo.die(owner)][:1])
    direct = list(near)
    for c in pick:
        if len(direct) > 1:
            kto[c] = direct.pop()
            vto[c] = kto[c]
    return owner, kto, vto, direct


def _ids(topo, dsts):
    return [DstId(rid=topo.addr(d)[0], pnc=topo.addr(d)[1]) for d in dsts]


def rank_program(g, core, T, topo):
    owner, kto, vto, direct = _plan(T, topo)
    rank = T.rank_of(core)
    sem = T.sem
    if rank is None and core not in kto:
        return
    relays = list(kto)
    on_chip = _common(topo, owner, relays)
    head = _halves(_halves(on_chip)[1])[1]
    off_chip = _common(topo, owner, direct)
    n_on, n_off = _count(on_chip), _count(off_chip)

    def write(src, dst, dsts, m, rsem):
        g.remote_dma_fused(
            [RemoteDMATransfer(dst_ids=_ids(topo, dsts), dma_engine_mask=m, remote_sem=rsem,
                               srcs=[src], dsts=[dst for _ in dsts])],
            local_sem=sem.sent)
        return _count(m)

    if core in kto:
        m = _common(topo, core, [kto[core], vto[core]])
        g.wait_ge(sem.hin, _count(head))
        left = write(T.vh[:, :], T.vh[:, :], [kto[core]], m, sem.hin)
        g.wait_ge(sem.k0in, n_on)
        left += write(T.kd0[:, :], T.kv[:, 0:128], [kto[core]], m, sem.k0in)
        g.wait_ge(sem.k1in, n_on)
        left += write(T.kd1[:, :], T.kv[:, 128:256], [kto[core]], m, sem.k1in)
        g.wait_ge(sem.v0in, n_on)
        left += write(T.vd0[:, :], T.kv[:, 256 + HEAD:384], [vto[core]], m, sem.v0in)
        g.wait_ge(sem.v1in, n_on)
        left += write(T.vd1[:, :], T.kv[:, 384:512], [vto[core]], m, sem.v1in)
        g.wait_ge(sem.sent, left)
        return

    if core == owner:
        g.sync.dma_start(T.vh[:, :], T.v[:, 0:HEAD]).then_inc(sem.hl, 16)
        g.sync.dma_start(T.kd0[:, :], T.k[:, 0:128]).then_inc(sem.kl0, 16)
        g.sync.dma_start(T.kd1[:, :], T.k[:, 128:256]).then_inc(sem.kl1, 16)
        g.sync.dma_start(T.kv[:, 0:256], T.k[:, :]).then_inc(sem.ksb, 16)
        g.scalar.wait_ge(sem.hl, 16)
        g.scalar.dma_start(T.vd0[:, :], T.v[:, HEAD:128]).then_inc(sem.vl0, 16)
        g.scalar.dma_start(T.vd1[:, :], T.v[:, 128:256]).then_inc(sem.vl1, 16)
        g.scalar.dma_start(T.kv[:, 256:512], T.v[:, :]).then_inc(sem.vsb, 16)
    g.sync.dma_start(T.qs[:, :], T.q[:, :]).then_inc(sem.qin, 16)
    g.vector.memset(T.zero[:, :], 0.0).then_inc(sem.zf, 1)

    if core == owner:
        g.wait_ge(sem.hl, 16)
        left = write(T.vh[:, :], T.vh[:, :], relays, head, sem.hin)
        g.wait_ge(sem.kl0, 16)
        left += write(T.kd0[:, :], T.kd0[:, :], relays, on_chip, sem.k0in)
        g.wait_ge(sem.kl1, 16)
        left += write(T.kd1[:, :], T.kd1[:, :], relays, on_chip, sem.k1in)
        g.wait_ge(sem.vl0, 16)
        left += write(T.vd0[:, :], T.vd0[:, :], relays, on_chip, sem.v0in)
        g.wait_ge(sem.vl1, 16)
        left += write(T.vd1[:, :], T.vd1[:, :], relays, on_chip, sem.v1in)
        g.wait_ge(sem.ksb, 16)
        left += write(T.kv[:, 0:256], T.kv[:, 0:256], direct, off_chip, sem.k0in)
        g.wait_ge(sem.vsb, 16)
        left += write(T.kv[:, 256:384], T.kv[:, 256:384], direct, off_chip, sem.v0in)
        left += write(T.kv[:, 384:512], T.kv[:, 384:512], direct, off_chip, sem.v1in)
        g.wait_ge(sem.sent, left)

    if core == owner:
        wk0, wk1, wv0, wv1 = [(sem.ksb, 16)], [], [(sem.vsb, 16)], []
    elif core in direct:
        wk0, wk1, wv0, wv1 = [(sem.k0in, n_off)], [], [(sem.v0in, n_off)], [(sem.v1in, n_off)]
    else:
        ks = [c for c in relays if kto[c] == core][0]
        vs = [c for c in relays if vto[c] == core][0]
        nk = _count(_common(topo, ks, [kto[ks], vto[ks]]))
        nv = _count(_common(topo, vs, [kto[vs], vto[vs]]))
        g.sync.wait_ge(sem.hin, nk)
        g.sync.dma_start(T.kv[:, 256:256 + HEAD], T.vh[:, :]).then_inc(sem.hsb, 16)
        wk0, wk1 = [(sem.k0in, nk)], [(sem.k1in, nk)]
        wv0, wv1 = [(sem.v0in, nv), (sem.hsb, 16)], [(sem.v1in, nv)]

    te, ve, se = g.tensor, g.vector, g.scalar
    k0, k1 = T.kv[:, 0:128], T.kv[:, 128:256]
    v0, v1 = T.kv[:, 256:384], T.kv[:, 384:512]
    relu = ActivationFunctionType.Relu
    te.wait_ge(sem.qin, 16)
    for s, n in wk0:
        te.wait_ge(s, n)
    te.matmul(T.ps00[:, 0:128], k0, T.qs[:, 0:128], True, True).then_inc(sem.a00, 1)
    te.matmul(T.ps01[:, 0:128], k0, T.qs[:, 128:256], True, True).then_inc(sem.a01, 1)
    for s, n in wk1:
        te.wait_ge(s, n)
    te.matmul(T.ps10[:, 0:128], k1, T.qs[:, 0:128], True, True).then_inc(sem.a10, 1)
    te.matmul(T.ps11[:, 0:128], k1, T.qs[:, 128:256], True, True).then_inc(sem.a11, 1)
    ve.wait_ge(sem.zf, 1)
    ve.wait_ge(sem.a00, 1)
    ve.tensor_tensor(T.s0[:, 0:128], T.ps00[:, 0:128], T.zero[:, :], AluOpType.max).then_inc(sem.r00, 1)
    se.wait_ge(sem.a01, 1)
    se.activation(T.s0[:, 128:256], T.ps01[:, 0:128], relu).then_inc(sem.r01, 1)
    ve.wait_ge(sem.a10, 1)
    ve.tensor_tensor(T.s1[:, 0:128], T.ps10[:, 0:128], T.zero[:, :], AluOpType.max).then_inc(sem.r10, 1)
    se.wait_ge(sem.a11, 1)
    se.activation(T.s1[:, 128:256], T.ps11[:, 0:128], relu).then_inc(sem.r11, 1)
    for s, n in wv0:
        te.wait_ge(s, n)
    te.wait_ge(sem.r00, 1)
    te.matmul(T.po0[:, 0:128], v0, T.s0[:, 0:128], True, False)
    te.wait_ge(sem.r01, 1)
    te.matmul(T.po1[:, 0:64], v0, T.s0[:, 128:192], True, False)
    te.matmul(T.po2[:, 0:64], v0, T.s0[:, 192:256], True, False)
    for s, n in wv1:
        te.wait_ge(s, n)
    te.wait_ge(sem.r10, 1)
    te.matmul(T.po0[:, 0:128], v1, T.s1[:, 0:128], False, True).then_inc(sem.od0, 1)
    te.wait_ge(sem.r11, 1)
    te.matmul(T.po1[:, 0:64], v1, T.s1[:, 128:192], False, True).then_inc(sem.od1, 1)
    te.matmul(T.po2[:, 0:64], v1, T.s1[:, 192:256], False, True).then_inc(sem.od2, 1)
    ve.wait_ge(sem.od0, 1)
    ve.tensor_copy(T.ys[:, 0:128], T.po0[:, 0:128]).then_inc(sem.cd0, 1)
    ve.wait_ge(sem.od1, 1)
    ve.tensor_copy(T.ys[:, 128:192], T.po1[:, 0:64]).then_inc(sem.cd1, 1)
    ve.wait_ge(sem.od2, 1)
    ve.tensor_copy(T.ys[:, 192:256], T.po2[:, 0:64]).then_inc(sem.cd1, 1)
    g.scalar.wait_ge(sem.cd0, 1)
    g.scalar.dma_start(T.y[:, 0:128], T.ys[:, 0:128]).then_inc(sem.st0, 16)
    g.sync.wait_ge(sem.cd1, 2)
    g.sync.dma_start(T.y[:, 128:256], T.ys[:, 128:256]).then_inc(sem.st1, 16)
    g.scalar.wait_ge(sem.st0, 16)
    g.sync.wait_ge(sem.st1, 16)
